import numpy as np
import ml_dtypes


def mxq(x, axis, fmt="e4m3"):
    dtype, down = {"e4m3": (ml_dtypes.float8_e4m3fn, 7), "e5m2": (ml_dtypes.float8_e5m2, 14)}[fmt]
    v = np.moveaxis(np.asarray(x, np.float32).astype(ml_dtypes.bfloat16).astype(np.float64), axis, -1)
    blocks = v.reshape(v.shape[:-1] + (-1, 32))
    amax = np.abs(blocks).max(-1, keepdims=True)
    byte = np.maximum(np.where(amax > 0, np.frexp(amax)[1] - 1 + 127, 0) - down, 1)
    scale = np.exp2(byte - 127.0)
    codes = (blocks / scale).astype(np.float32).astype(dtype).astype(np.float64)
    return np.moveaxis((codes * scale).reshape(v.shape), -1, axis)


WIDE = False


def mx_kscale(k):
    if not WIDE:
        return np.ones(k)
    levels = np.array([10, -10, 5, -5, 0])
    if k % 512:
        return np.exp2(np.random.permutation(np.resize(levels, k // 32))).repeat(32)
    a = np.empty((k // 512, 16))
    for p in range(k // 512):
        a[p, :8] = np.random.permutation(np.resize(levels, 8))
        for g in range(8):
            far = levels[np.abs(levels - a[p, g]) >= 10]
            a[p, g + 8] = far[np.random.randint(len(far))]
    return np.exp2(a.ravel()).repeat(32)


def f64(x):
    return np.asarray(x).astype(np.float64)


def striped(idx):
    return np.tile(idx.reshape(-1, 16).T, (8, 1)).astype(np.uint16)


def unstriped(offs):
    return offs[:16].T.reshape(-1).astype(np.int64)


def relu(v):
    return np.maximum(v, 0.0)

def planes(y):
    n, m = y.shape
    v = y.astype(np.float32).astype(ml_dtypes.bfloat16).astype(np.float64).reshape(n // 32, 32, m)
    top = np.abs(v).max(1)
    byte = np.clip(np.where(top > 0, np.frexp(top)[1] - 1 + 127 - 7, 1), 1, 254)
    codes = (v * np.exp2(127.0 - byte)[:, None, :]).reshape(n, m).astype(np.float32).astype(ml_dtypes.float8_e4m3fn).view(np.uint8)
    words = codes.reshape(n // 512, 128, 4, m).transpose(0, 1, 3, 2)
    return np.ascontiguousarray(words), np.ascontiguousarray(byte.astype(np.uint8).reshape(n // 512, 16, m))


K, T, S, H, U = 512, 2048, 1024, 512, 1024


def setup_inputs():
    n = np.random.standard_normal
    s = mx_kscale(K)[:, None]
    u = mx_kscale(H)
    return {
        "xT": (n((K, T)) * s).astype(np.float32),
        "w1": (n((K, H)) / np.sqrt(2 * K) / s * u).astype(np.float32),
        "w2": (n((K, H)) / np.sqrt(2 * K) / s * u).astype(np.float32),
        "w3": (n((H, H)) / np.sqrt(H) / u[:, None]).astype(np.float32),
        "offs": striped(np.random.permutation(T)[:S]),
        "src": striped(np.random.permutation(S)[(S * np.random.uniform(0, 1, U) ** 4).astype(np.int64)]),
        "dst": striped(np.random.permutation(S)),
    }


def reference(xT, w1, w2, w3, offs, src, dst):
    xq = mxq(f64(xT)[:, unstriped(offs)], 0, "e4m3")
    y = mxq(f64(w1), 0, "e4m3").T @ xq
    e = mxq(f64(w2), 0, "e4m3").T @ xq
    z = relu(y[:, unstriped(src)] + e[:, unstriped(dst)])
    out_0 = mxq(f64(w3), 0, "e4m3").T @ mxq(z, 0, "e4m3")
    return (out_0,) + planes(out_0)

@@ -1,0 +1,223 @@
+from contextlib import ExitStack
+
+import concourse.mybir as mybir
+
+K, T, S, H = 512, 2048, 1024, 512
+FLOPS = 3 * 2 * K * H * S
+
+F32 = mybir.dt.float32
+BF16 = mybir.dt.bfloat16
+U32 = mybir.dt.uint32
+I32 = mybir.dt.int32
+U16 = mybir.dt.uint16
+U8 = mybir.dt.uint8
+FP8X4 = mybir.dt.float8_e4m3fn_x4
+ADD = mybir.AluOpType.add
+RELU = mybir.ActivationFunctionType.Relu
+COPY = mybir.ActivationFunctionType.Copy
+
+P = 128
+PACK = 4
+HALF = 512
+OUT_BLOCK = 128
+
+
+def tile_picked_hub_relu_lo_kernel(tc, xT, w1, w2, w3, offs, src, dst, out_0, out_1, out_2):
+    nc = tc.nc
+    with ExitStack() as ctx:
+        lists = ctx.enter_context(tc.tile_pool(name="lists", bufs=1))
+        pool = ctx.enter_context(tc.tile_pool(name="pool", bufs=1))
+        psum = ctx.enter_context(tc.psum_pool(name="psum", bufs=4))
+
+        def sbuf(shape, dtype, name, tag=None):
+            return pool.tile(shape, dtype, name=name, tag=tag or name, align_bytes=64)
+
+        def entries(list_tile, first, count):
+            return list_tile[:, first // 16 : (first + count) // 16]
+
+        def quantize(name, values, width):
+            codes = sbuf([P, width], U32, name + "_codes")
+            scales = sbuf([P, width], U8, name + "_scales")
+            nc.vector.quantize_mx(out=codes[:].bitcast(FP8X4), scales=scales[:], in_=values)
+            return codes, scales
+
+        def product(out, stationary, t, moving, cols):
+            m = slice(P * t, P * (t + 1))
+            nc.tensor.matmul_mx(
+                out=out,
+                lhsT=stationary[0][:, m].bitcast(FP8X4),
+                lhsT_scale=stationary[1][:, m],
+                rhs=moving[0][:, cols].bitcast(FP8X4),
+                rhs_scale=moving[1][:, cols],
+                start=True,
+                stop=True,
+            )
+
+        x_rows = xT.rearrange("(p j) n -> p j n", j=PACK)
+        offs_t = lists.tile([P, S // 16], U16, name="offs_t")
+        src_t = lists.tile([P, S // 16], U16, name="src_t")
+        dst_t = lists.tile([P, S // 16], U16, name="dst_t")
+        x_chunks = [(0, 0, 1024), (0, 1024, 1024)] + [(1, c, 512) for c in range(0, T, 512)]
+        raw = []
+        for n, (u, first, width) in enumerate(x_chunks):
+            chunk = sbuf([P, 2, width], F32, "x_raw%d" % n)
+            nc.sync.dma_start(out=chunk[:], in_=x_rows[:, 2 * u : 2 * u + 2, first : first + width])
+            raw.append(chunk)
+            if n == 0:
+                nc.sync.dma_start(offs_t[:], offs)
+        w_raw = []
+        for n, w in enumerate((w1, w2, w3)):
+            rows = sbuf([P, PACK, H], F32, "w_raw%d" % n)
+            nc.sync.dma_start(out=rows[:], in_=w.rearrange("(p j) c -> p j c", j=PACK))
+            w_raw.append(rows)
+            if n == 0:
+                nc.sync.dma_start(src_t[:], src)
+                nc.sync.dma_start(dst_t[:], dst)
+
+        pairs = [sbuf([P, 2 * T], BF16, "pairs%d" % u) for u in range(2)]
+        picked = [sbuf([P, PACK * HALF], BF16, "picked%d" % h) for h in range(2)]
+
+        def gather_x(u, h):
+            nc.vector.tensor_copy(
+                picked[h][:].bitcast(U32)[:, u::2],
+                pairs[u][:].bitcast(U32).indirect(entries(offs_t, HALF * h, HALF)),
+            )
+
+        for n, (u, first, width) in enumerate(x_chunks):
+            paired = pairs[u][:, 2 * first : 2 * (first + width)].rearrange("p (n e) -> p n e", e=2)
+            source = raw[n][:].rearrange("p e n -> p n e")
+            if first + width == T:
+                nc.vector.tensor_copy(paired, source)
+            else:
+                nc.scalar.copy(paired, source)
+            if (u, first + width) == (0, T):
+                gather_x(0, 0)
+                gather_x(0, 1)
+
+        def round_weights(n):
+            dealt = sbuf([P, PACK * H], BF16, "w_dealt%d" % n, tag="w_dealt")
+            return (
+                dealt,
+                dealt[:].rearrange("p (t m j) -> p m j t", t=PACK, j=PACK),
+                w_raw[n][:].rearrange("p j (m t) -> p m j t", t=PACK),
+            )
+
+        w1_dealt, to, of = round_weights(0)
+        nc.scalar.activation(to, of, COPY)
+        gather_x(1, 0)
+        gather_x(1, 1)
+        xq = [quantize("x0", picked[0][:], HALF)]
+        w1q = quantize("w1", w1_dealt[:], H)
+        xq.append(quantize("x1", picked[1][:], HALF))
+        w2_dealt, to, of = round_weights(1)
+        nc.vector.tensor_copy(to, of)
+        w2q = quantize("w2", w2_dealt[:], H)
+
+        def first_layer(name, wq):
+            rows = []
+            for t in range(PACK):
+                row = sbuf([P, S], F32, "%s%d" % (name, t))
+                for h in range(2):
+                    bank = psum.tile([P, HALF], F32, name="first_bank")
+                    product(bank[:], wq, t, xq[h], slice(0, HALF))
+                    nc.scalar.copy(row[:, HALF * h : HALF * (h + 1)], bank[:])
+                rows.append(row)
+            return rows
+
+        y = first_layer("y", w1q)
+        e = first_layer("e", w2q)
+        w3_dealt, to, of = round_weights(2)
+        nc.scalar.copy(to, of)
+
+        def gather_sources(into, ts, first, count):
+            for n, t in enumerate(ts):
+                nc.vector.tensor_copy(into[:, n, :], y[t][:].indirect(entries(src_t, first, count)))
+
+        def add_targets(into, t, fetched, first, count):
+            nc.vector.tensor_tensor(into[:, t, :], e[t][:].indirect(entries(dst_t, first, count)), fetched, ADD)
+
+        def relu_views(z_bf, z, first, count):
+            return (
+                z_bf[:].rearrange("p (c i t) -> p c t i", i=4, t=PACK),
+                z[:, :, first : first + count].rearrange("p t (c i) -> p c t i", i=4),
+            )
+
+        out_rows = out_0.rearrange("(p t) r -> p t r", t=PACK)
+        out_words = out_1.rearrange("z p c r -> (z p) (c r)").bitcast(I32)
+        out_scale_rows = out_2.rearrange("z q c -> (z q) c").bitcast(I32)
+        out_codes = sbuf([P, S], U32, "out_codes")
+        out_scales = sbuf([P, S], U8, "out_scales")
+
+        def second_layer(name, zq, first, count, tag, round_on_vector=False, queue=nc.sync):
+            result = sbuf([P, PACK, count], F32, name + "_result")
+            rounded = sbuf([P, PACK * count], BF16, name + "_rounded", tag=tag)
+            for c in range(0, count, OUT_BLOCK):
+                bank = psum.tile([P, PACK, OUT_BLOCK], F32, name="second_bank")
+                for t in range(PACK):
+                    product(bank[:, t, :], w3q, t, zq, slice(c, c + OUT_BLOCK))
+                to = rounded[:, PACK * c : PACK * (c + OUT_BLOCK)].rearrange("p (n t) -> p n t", t=PACK)
+                if round_on_vector:
+                    nc.vector.tensor_copy(to, bank[:].rearrange("p t n -> p n t"))
+                else:
+                    nc.scalar.copy(to, bank[:].rearrange("p t n -> p n t"))
+                nc.scalar.copy(result[:, :, c : c + OUT_BLOCK], bank[:])
+            queue.dma_start(out=out_rows[:, :, first : first + count], in_=result[:])
+            return rounded
+
+        def quantize_out(rounded, first, count):
+            cols = slice(first, first + count)
+            nc.vector.quantize_mx(out=out_codes[:, cols].bitcast(FP8X4), scales=out_scales[:, cols], in_=rounded[:])
+            nc.sync.dma_start(out=out_words[:, cols], in_=out_codes[:, cols].bitcast(I32))
+
+        g_a = sbuf([P, PACK, 512], F32, "g_a", tag="G")
+        z_a = sbuf([P, PACK, 512], F32, "z_a", tag="Z")
+        gather_sources(g_a, range(PACK), 0, 512)
+        for t in range(PACK):
+            add_targets(z_a, t, g_a[:, t, :], 0, 512)
+        w3q = quantize("w3", w3_dealt[:], H)
+        zb0 = sbuf([P, 1024], BF16, "zb0", tag="X0")
+        zb1 = sbuf([P, 1024], BF16, "zb1", tag="X1")
+        nc.scalar.activation(*relu_views(zb0, z_a, 0, 256), RELU)
+        nc.scalar.activation(*relu_views(zb1, z_a, 256, 256), RELU)
+        g2a = sbuf([P, 2, 256], F32, "g2a", tag="G")
+        gather_sources(g2a, (0, 1), 512, 256)
+        zq0 = quantize("z0", zb0[:], 256)
+        g2b = sbuf([P, 2, 256], F32, "g2b", tag="X0")
+        gather_sources(g2b, (2, 3), 512, 256)
+        zq1 = quantize("z1", zb1[:], 256)
+        ob0 = second_layer("o0", zq0, 0, 256, "O0")
+        ob1 = second_layer("o1", zq1, 256, 256, "O1")
+        z2 = sbuf([P, PACK, 256], F32, "z2", tag="X1")
+        for t in range(PACK):
+            add_targets(z2, t, (g2a, g2b)[t // 2][:, t % 2, :], 512, 256)
+        zb2 = sbuf([P, 1024], BF16, "zb2", tag="Z")
+        nc.scalar.activation(*relu_views(zb2, z2, 0, 256), RELU)
+        g3a = sbuf([P, 2, 256], F32, "g3a", tag="X0")
+        gather_sources(g3a, (0, 1), 768, 256)
+        quantize_out(ob0, 0, 256)
+        g3b = sbuf([P, 2, 256], F32, "g3b", tag="O0")
+        gather_sources(g3b, (2, 3), 768, 256)
+        zq2 = quantize("z2", zb2[:], 256)
+        quantize_out(ob1, 256, 256)
+        ob2 = second_layer("o2", zq2, 512, 256, "O2")
+        z3a = sbuf([P, PACK, 128], F32, "z3a", tag="Z")
+        for t in range(PACK):
+            add_targets(z3a, t, (g3a, g3b)[t // 2][:, t % 2, 0:128], 768, 128)
+        zb3a = sbuf([P, 512], BF16, "zb3a")
+        nc.scalar.activation(*relu_views(zb3a, z3a, 0, 128), RELU)
+        z3b = sbuf([P, PACK, 128], F32, "z3b", tag="O1")
+        for t in range(PACK):
+            add_targets(z3b, t, (g3a, g3b)[t // 2][:, t % 2, 128:256], 896, 128)
+        zq3a = quantize("z3a", zb3a[:], 128)
+        zb3b = sbuf([P, 512], BF16, "zb3b")
+        to, of = relu_views(zb3b, z3b, 0, 128)
+        nc.vector.tensor_scalar_max(to, of, 0.0)
+        quantize_out(ob2, 512, 256)
+        zq3b = quantize("z3b", zb3b[:], 128)
+        ob3a = second_layer("o3a", zq3a, 768, 128, "O3a")
+        ob3b = second_layer("o3b", zq3b, 896, 128, "O3b", round_on_vector=True, queue=nc.scalar)
+        quantize_out(ob3a, 768, 128)
+        quantize_out(ob3b, 896, 128)
+        for q in range(4):
+            queue = nc.sync if q < 2 else nc.scalar
+            queue.dma_start(out=out_scale_rows[4 * q : 4 * q + 4, :], in_=out_scales[32 * q : 32 * q + 4, :].bitcast(I32))

@@ -27,19 +27,35 @@ def tile_picked_hub_relu_lo_kernel(tc, xT, w1, w2, w3, offs, src, dst, out_0, ou
     with ExitStack() as ctx:
         lists = ctx.enter_context(tc.tile_pool(name="lists", bufs=1))
         pool = ctx.enter_context(tc.tile_pool(name="pool", bufs=1))
+        staged = ctx.enter_context(tc.tile_pool(name="staged", bufs=1))
         psum = ctx.enter_context(tc.psum_pool(name="psum", bufs=4))
 
         def sbuf(shape, dtype, name, tag=None):
             return pool.tile(shape, dtype, name=name, tag=tag or name, align_bytes=64)
 
+        def placed(shape, dtype, name, offset):
+            return staged.tile(shape, dtype, name=name, align_bytes=64, offset=offset)
+
         def entries(list_tile, first, count):
             return list_tile[:, first // 16 : (first + count) // 16]
 
-        def quantize(name, values, width):
+        def mx_tiles(name, width):
             codes = sbuf([P, width], U32, name + "_codes")
             scales = sbuf([P, width], U8, name + "_scales")
-            nc.vector.quantize_mx(out=codes[:].bitcast(FP8X4), scales=scales[:], in_=values)
             return codes, scales
+
+        def quantize_part(operand, values, first, count):
+            cols = slice(first, first + count)
+            nc.vector.quantize_mx(
+                out=operand[0][:, cols].bitcast(FP8X4),
+                scales=operand[1][:, cols],
+                in_=values[:, PACK * first : PACK * (first + count)],
+            )
+
+        def quantize(name, values, width):
+            operand = mx_tiles(name, width)
+            quantize_part(operand, values, 0, width)
+            return operand
 
         def product(out, stationary, t, moving, cols):
             m = slice(P * t, P * (t + 1))
@@ -57,22 +73,26 @@ def tile_picked_hub_relu_lo_kernel(tc, xT, w1, w2, w3, offs, src, dst, out_0, ou
         offs_t = lists.tile([P, S // 16], U16, name="offs_t")
         src_t = lists.tile([P, S // 16], U16, name="src_t")
         dst_t = lists.tile([P, S // 16], U16, name="dst_t")
-        x_chunks = [(0, 0, 1024), (0, 1024, 1024)] + [(1, c, 512) for c in range(0, T, 512)]
+        x_chunks = [(0, 0, 1024, 1024), (0, 1024, 1024, 320), (1, 0, 1024, 1024), (1, 1024, 512, 0), (1, 1536, 512, 160)]
         raw = []
-        for n, (u, first, width) in enumerate(x_chunks):
+        for n, (u, first, width, on_scalar) in enumerate(x_chunks):
             chunk = sbuf([P, 2, width], F32, "x_raw%d" % n)
             nc.sync.dma_start(out=chunk[:], in_=x_rows[:, 2 * u : 2 * u + 2, first : first + width])
             raw.append(chunk)
             if n == 0:
                 nc.sync.dma_start(offs_t[:], offs)
-        w_raw = []
-        for n, w in enumerate((w1, w2, w3)):
-            rows = sbuf([P, PACK, H], F32, "w_raw%d" % n)
-            nc.sync.dma_start(out=rows[:], in_=w.rearrange("(p j) c -> p j c", j=PACK))
-            w_raw.append(rows)
-            if n == 0:
-                nc.sync.dma_start(src_t[:], src)
-                nc.sync.dma_start(dst_t[:], dst)
+        w1_rows = w1.rearrange("(p j) c -> p j c", j=PACK)
+        w1_raw = []
+        for n in range(2):
+            rows = sbuf([P, PACK, H // 2], F32, "w1_raw%d" % n)
+            nc.sync.dma_start(out=rows[:], in_=w1_rows[:, :, H // 2 * n : H // 2 * (n + 1)])
+            w1_raw.append(rows)
+        nc.sync.dma_start(src_t[:], src)
+        w2_raw = sbuf([P, PACK, H], F32, "w2_raw")
+        nc.sync.dma_start(out=w2_raw[:], in_=w2.rearrange("(p j) c -> p j c", j=PACK))
+        nc.sync.dma_start(dst_t[:], dst)
+        w3_raw = sbuf([P, PACK, H], F32, "w3_raw")
+        nc.sync.dma_start(out=w3_raw[:], in_=w3.rearrange("(p j) c -> p j c", j=PACK))
 
         pairs = [sbuf([P, 2 * T], BF16, "pairs%d" % u) for u in range(2)]
         picked = [sbuf([P, PACK * HALF], BF16, "picked%d" % h) for h in range(2)]
@@ -83,35 +103,42 @@ def tile_picked_hub_relu_lo_kernel(tc, xT, w1, w2, w3, offs, src, dst, out_0, ou
                 pairs[u][:].bitcast(U32).indirect(entries(offs_t, HALF * h, HALF)),
             )
 
-        for n, (u, first, width) in enumerate(x_chunks):
-            paired = pairs[u][:, 2 * first : 2 * (first + width)].rearrange("p (n e) -> p n e", e=2)
-            source = raw[n][:].rearrange("p e n -> p n e")
-            if first + width == T:
-                nc.vector.tensor_copy(paired, source)
-            else:
-                nc.scalar.copy(paired, source)
+        def pair_views(n, a, b):
+            u, first = x_chunks[n][:2]
+            return (
+                pairs[u][:, 2 * (first + a) : 2 * (first + b)].rearrange("p (c i e) -> p c e i", i=4, e=2),
+                raw[n][:, :, a:b].rearrange("p e (c i) -> p c e i", i=4),
+            )
+
+        for n, (u, first, width, on_scalar) in enumerate(x_chunks):
+            if on_scalar:
+                nc.scalar.copy(*pair_views(n, 0, on_scalar))
+            if on_scalar < width:
+                nc.vector.tensor_copy(*pair_views(n, on_scalar, width))
             if (u, first + width) == (0, T):
                 gather_x(0, 0)
                 gather_x(0, 1)
 
-        def round_weights(n):
-            dealt = sbuf([P, PACK * H], BF16, "w_dealt%d" % n, tag="w_dealt")
+        def dealt_views(dealt, rows, m0, m1):
             return (
-                dealt,
-                dealt[:].rearrange("p (t m j) -> p m j t", t=PACK, j=PACK),
-                w_raw[n][:].rearrange("p j (m t) -> p m j t", t=PACK),
+                dealt[:].rearrange("p (t m j) -> p m j t", t=PACK, j=PACK)[:, m0:m1],
+                rows[:].rearrange("p j (m t) -> p m j t", t=PACK),
             )
 
-        w1_dealt, to, of = round_weights(0)
-        nc.scalar.activation(to, of, COPY)
+        w1_dealt = sbuf([P, PACK * H], BF16, "w1_dealt", tag="w_dealt")
+        for n in range(2):
+            nc.scalar.activation(*dealt_views(w1_dealt, w1_raw[n], 64 * n, 64 * (n + 1)), COPY)
         gather_x(1, 0)
         gather_x(1, 1)
-        xq = [quantize("x0", picked[0][:], HALF)]
-        w1q = quantize("w1", w1_dealt[:], H)
-        xq.append(quantize("x1", picked[1][:], HALF))
-        w2_dealt, to, of = round_weights(1)
-        nc.vector.tensor_copy(to, of)
-        w2q = quantize("w2", w2_dealt[:], H)
+        xq = [quantize("x0", picked[0], HALF)]
+        w1q = mx_tiles("w1", H)
+        quantize_part(w1q, w1_dealt, 0, 128)
+        xq.append(quantize("x1", picked[1], HALF))
+        quantize_part(w1q, w1_dealt, 128, 128)
+        quantize_part(w1q, w1_dealt, 256, 256)
+        w2_dealt = sbuf([P, PACK * H], BF16, "w2_dealt", tag="w_dealt")
+        nc.vector.tensor_copy(*dealt_views(w2_dealt, w2_raw, 0, P))
+        w2q = quantize("w2", w2_dealt, H)
 
         def first_layer(name, wq):
             rows = []
@@ -126,8 +153,8 @@ def tile_picked_hub_relu_lo_kernel(tc, xT, w1, w2, w3, offs, src, dst, out_0, ou
 
         y = first_layer("y", w1q)
         e = first_layer("e", w2q)
-        w3_dealt, to, of = round_weights(2)
-        nc.scalar.copy(to, of)
+        w3_dealt = sbuf([P, PACK * H], BF16, "w3_dealt", tag="w_dealt")
+        nc.scalar.copy(*dealt_views(w3_dealt, w3_raw, 0, P))
 
         def gather_sources(into, ts, first, count):
             for n, t in enumerate(ts):
@@ -145,79 +172,82 @@ def tile_picked_hub_relu_lo_kernel(tc, xT, w1, w2, w3, offs, src, dst, out_0, ou
         out_rows = out_0.rearrange("(p t) r -> p t r", t=PACK)
         out_words = out_1.rearrange("z p c r -> (z p) (c r)").bitcast(I32)
         out_scale_rows = out_2.rearrange("z q c -> (z q) c").bitcast(I32)
-        out_codes = sbuf([P, S], U32, "out_codes")
         out_scales = sbuf([P, S], U8, "out_scales")
 
-        def second_layer(name, zq, first, count, tag, round_on_vector=False, queue=nc.sync):
+        def second_layer(name, zq, first, count, rounded, round_on_vector=False, queue=nc.sync):
             result = sbuf([P, PACK, count], F32, name + "_result")
-            rounded = sbuf([P, PACK * count], BF16, name + "_rounded", tag=tag)
             for c in range(0, count, OUT_BLOCK):
                 bank = psum.tile([P, PACK, OUT_BLOCK], F32, name="second_bank")
                 for t in range(PACK):
                     product(bank[:, t, :], w3q, t, zq, slice(c, c + OUT_BLOCK))
-                to = rounded[:, PACK * c : PACK * (c + OUT_BLOCK)].rearrange("p (n t) -> p n t", t=PACK)
+                to = rounded[:, PACK * c : PACK * (c + OUT_BLOCK)].rearrange("p (c i t) -> p c t i", i=4, t=PACK)
+                of = bank[:].rearrange("p t (c i) -> p c t i", i=4)
                 if round_on_vector:
-                    nc.vector.tensor_copy(to, bank[:].rearrange("p t n -> p n t"))
+                    nc.vector.tensor_copy(to, of)
                 else:
-                    nc.scalar.copy(to, bank[:].rearrange("p t n -> p n t"))
+                    nc.scalar.copy(to, of)
                 nc.scalar.copy(result[:, :, c : c + OUT_BLOCK], bank[:])
             queue.dma_start(out=out_rows[:, :, first : first + count], in_=result[:])
-            return rounded
 
-        def quantize_out(rounded, first, count):
+        def quantize_out(codes, rounded, first, count):
             cols = slice(first, first + count)
-            nc.vector.quantize_mx(out=out_codes[:, cols].bitcast(FP8X4), scales=out_scales[:, cols], in_=rounded[:])
-            nc.sync.dma_start(out=out_words[:, cols], in_=out_codes[:, cols].bitcast(I32))
+            nc.vector.quantize_mx(out=codes[:].bitcast(FP8X4), scales=out_scales[:, cols], in_=rounded[:])
+            nc.sync.dma_start(out=out_words[:, cols], in_=codes[:].bitcast(I32))
 
-        g_a = sbuf([P, PACK, 512], F32, "g_a", tag="G")
-        z_a = sbuf([P, PACK, 512], F32, "z_a", tag="Z")
-        gather_sources(g_a, range(PACK), 0, 512)
+        g_a = sbuf([P, 3, 512], F32, "g_a")
+        gather_sources(g_a, range(3), 0, 512)
+        g03 = sbuf([P, 1, 256], F32, "g03", tag="A")
+        g13 = sbuf([P, 1, 256], F32, "g13")
+        gather_sources(g03, (3,), 0, 256)
+        gather_sources(g13, (3,), 256, 256)
+        z0 = sbuf([P, PACK, 256], F32, "z0")
         for t in range(PACK):
-            add_targets(z_a, t, g_a[:, t, :], 0, 512)
-        w3q = quantize("w3", w3_dealt[:], H)
-        zb0 = sbuf([P, 1024], BF16, "zb0", tag="X0")
-        zb1 = sbuf([P, 1024], BF16, "zb1", tag="X1")
-        nc.scalar.activation(*relu_views(zb0, z_a, 0, 256), RELU)
-        nc.scalar.activation(*relu_views(zb1, z_a, 256, 256), RELU)
-        g2a = sbuf([P, 2, 256], F32, "g2a", tag="G")
+            add_targets(z0, t, g_a[:, t, 0:256] if t < 3 else g03[:, 0, :], 0, 256)
+        z1 = sbuf([P, PACK, 256], F32, "z1", tag="A")
+        for t in range(PACK):
+            add_targets(z1, t, g_a[:, t, 256:512] if t < 3 else g13[:, 0, :], 256, 256)
+        w3q = quantize("w3", w3_dealt, H)
+        zb0 = sbuf([P, 1024], BF16, "zb0", tag="B")
+        zb1 = placed([P, 1024], BF16, "zb1", 3072)
+        nc.scalar.activation(*relu_views(zb0, z0, 0, 256), RELU)
+        nc.scalar.activation(*relu_views(zb1, z1, 0, 256), RELU)
+        zq0 = quantize("z0", zb0, 256)
+        g2a = sbuf([P, 2, 256], F32, "g2a", tag="B")
         gather_sources(g2a, (0, 1), 512, 256)
-        zq0 = quantize("z0", zb0[:], 256)
-        g2b = sbuf([P, 2, 256], F32, "g2b", tag="X0")
+        zq1 = quantize("z1", zb1, 256)
+        g2b = placed([P, 2, 256], F32, "g2b", 4096)
         gather_sources(g2b, (2, 3), 512, 256)
-        zq1 = quantize("z1", zb1[:], 256)
-        ob0 = second_layer("o0", zq0, 0, 256, "O0")
-        ob1 = second_layer("o1", zq1, 256, 256, "O1")
-        z2 = sbuf([P, PACK, 256], F32, "z2", tag="X1")
+        ob01 = sbuf([P, PACK * 512], BF16, "ob01")
+        second_layer("o0", zq0, 0, 256, ob01[:, 0:1024])
+        second_layer("o1", zq1, 256, 256, ob01[:, 1024:2048])
+        z2 = placed([P, PACK, 256], F32, "z2", 0)
         for t in range(PACK):
             add_targets(z2, t, (g2a, g2b)[t // 2][:, t % 2, :], 512, 256)
-        zb2 = sbuf([P, 1024], BF16, "zb2", tag="Z")
+        zb2 = placed([P, 1024], BF16, "zb2", 11264)
         nc.scalar.activation(*relu_views(zb2, z2, 0, 256), RELU)
-        g3a = sbuf([P, 2, 256], F32, "g3a", tag="X0")
+        g3a = placed([P, 2, 256], F32, "g3a", 4096)
         gather_sources(g3a, (0, 1), 768, 256)
-        quantize_out(ob0, 0, 256)
-        g3b = sbuf([P, 2, 256], F32, "g3b", tag="O0")
+        zq2 = quantize("z2", zb2, 256)
+        g3b = placed([P, 2, 256], F32, "g3b", 12288)
         gather_sources(g3b, (2, 3), 768, 256)
-        zq2 = quantize("z2", zb2[:], 256)
-        quantize_out(ob1, 256, 256)
-        ob2 = second_layer("o2", zq2, 512, 256, "O2")
-        z3a = sbuf([P, PACK, 128], F32, "z3a", tag="Z")
-        for t in range(PACK):
-            add_targets(z3a, t, (g3a, g3b)[t // 2][:, t % 2, 0:128], 768, 128)
-        zb3a = sbuf([P, 512], BF16, "zb3a")
-        nc.scalar.activation(*relu_views(zb3a, z3a, 0, 128), RELU)
-        z3b = sbuf([P, PACK, 128], F32, "z3b", tag="O1")
-        for t in range(PACK):
-            add_targets(z3b, t, (g3a, g3b)[t // 2][:, t % 2, 128:256], 896, 128)
-        zq3a = quantize("z3a", zb3a[:], 128)
-        zb3b = sbuf([P, 512], BF16, "zb3b")
-        to, of = relu_views(zb3b, z3b, 0, 128)
-        nc.vector.tensor_scalar_max(to, of, 0.0)
-        quantize_out(ob2, 512, 256)
-        zq3b = quantize("z3b", zb3b[:], 128)
-        ob3a = second_layer("o3a", zq3a, 768, 128, "O3a")
-        ob3b = second_layer("o3b", zq3b, 896, 128, "O3b", round_on_vector=True, queue=nc.scalar)
-        quantize_out(ob3a, 768, 128)
-        quantize_out(ob3b, 896, 128)
+        ob2 = sbuf([P, PACK * 256], BF16, "ob2")
+        second_layer("o2", zq2, 512, 256, ob2)
+        z3 = placed([P, PACK, 256], F32, "z3", 8192)
+        zb3 = []
+        for n in range(2):
+            for t in range(PACK):
+                cols = slice(128 * n, 128 * (n + 1))
+                add_targets(z3[:, :, cols], t, (g3a, g3b)[t // 2][:, t % 2, cols], 768 + 128 * n, 128)
+            zb3.append(sbuf([P, 512], BF16, "zb3_%d" % n))
+            nc.scalar.activation(*relu_views(zb3[n], z3, 128 * n, 128), RELU)
+        zq3a = quantize("z3a", zb3[0], 128)
+        quantize_out(placed([P, 512], U32, "codes01", 4096), ob01, 0, 512)
+        zq3b = quantize("z3b", zb3[1], 128)
+        quantize_out(placed([P, 256], U32, "codes2", 12288), ob2, 512, 256)
+        ob3 = sbuf([P, PACK * 256], BF16, "ob3")
+        second_layer("o3a", zq3a, 768, 128, ob3[:, 0:512])
+        second_layer("o3b", zq3b, 896, 128, ob3[:, 512:1024], round_on_vector=True, queue=nc.scalar)
+        quantize_out(sbuf([P, 256], U32, "codes3"), ob3, 768, 256)
         for q in range(4):
             queue = nc.sync if q < 2 else nc.scalar
             queue.dma_start(out=out_scale_rows[4 * q : 4 * q + 4, :], in_=out_scales[32 * q : 32 * q + 4, :].bitcast(I32))

@@ -39,8 +39,8 @@ def tile_picked_hub_relu_lo_kernel(tc, xT, w1, w2, w3, offs, src, dst, out_0, ou
         def entries(list_tile, first, count):
             return list_tile[:, first // 16 : (first + count) // 16]
 
-        def mx_tiles(name, width):
-            codes = sbuf([P, width], U32, name + "_codes")
+        def mx_tiles(name, width, tag=None):
+            codes = sbuf([P, width], U32, name + "_codes", tag=tag)
             scales = sbuf([P, width], U8, name + "_scales")
             return codes, scales
 
@@ -52,8 +52,8 @@ def tile_picked_hub_relu_lo_kernel(tc, xT, w1, w2, w3, offs, src, dst, out_0, ou
                 in_=values[:, PACK * first : PACK * (first + count)],
             )
 
-        def quantize(name, values, width):
-            operand = mx_tiles(name, width)
+        def quantize(name, values, width, tag=None):
+            operand = mx_tiles(name, width, tag)
             quantize_part(operand, values, 0, width)
             return operand
 
@@ -91,8 +91,10 @@ def tile_picked_hub_relu_lo_kernel(tc, xT, w1, w2, w3, offs, src, dst, out_0, ou
         w2_raw = sbuf([P, PACK, H], F32, "w2_raw")
         nc.sync.dma_start(out=w2_raw[:], in_=w2.rearrange("(p j) c -> p j c", j=PACK))
         nc.sync.dma_start(dst_t[:], dst)
-        w3_raw = sbuf([P, PACK, H], F32, "w3_raw")
-        nc.sync.dma_start(out=w3_raw[:], in_=w3.rearrange("(p j) c -> p j c", j=PACK))
+        w3_raw = placed([P, PACK, H], F32, "w3_raw", 0)
+        w3_rows = w3.rearrange("(g t b) c -> b g t c", t=PACK, b=2)
+        for b in range(2):
+            nc.sync.dma_start(out=w3_raw[b::2], in_=w3_rows[b])
 
         pairs = [sbuf([P, 2 * T], BF16, "pairs%d" % u) for u in range(2)]
         picked = [sbuf([P, PACK * HALF], BF16, "picked%d" % h) for h in range(2)]
@@ -125,9 +127,15 @@ def tile_picked_hub_relu_lo_kernel(tc, xT, w1, w2, w3, offs, src, dst, out_0, ou
                 rows[:].rearrange("p j (m t) -> p m j t", t=PACK),
             )
 
+        def hidden_views(dealt, rows, g0, g1):
+            return (
+                dealt[:].rearrange("p (t g b j) -> p g t j b", t=PACK, b=2, j=PACK)[:, g0:g1],
+                rows[:].rearrange("p j (g t b) -> p g t j b", t=PACK, b=2),
+            )
+
         w1_dealt = sbuf([P, PACK * H], BF16, "w1_dealt", tag="w_dealt")
         for n in range(2):
-            nc.scalar.activation(*dealt_views(w1_dealt, w1_raw[n], 64 * n, 64 * (n + 1)), COPY)
+            nc.scalar.copy(*hidden_views(w1_dealt, w1_raw[n], 32 * n, 32 * (n + 1)))
         gather_x(1, 0)
         gather_x(1, 1)
         xq = [quantize("x0", picked[0], HALF)]
@@ -137,7 +145,7 @@ def tile_picked_hub_relu_lo_kernel(tc, xT, w1, w2, w3, offs, src, dst, out_0, ou
         quantize_part(w1q, w1_dealt, 128, 128)
         quantize_part(w1q, w1_dealt, 256, 256)
         w2_dealt = sbuf([P, PACK * H], BF16, "w2_dealt", tag="w_dealt")
-        nc.vector.tensor_copy(*dealt_views(w2_dealt, w2_raw, 0, P))
+        nc.vector.tensor_copy(*hidden_views(w2_dealt, w2_raw, 0, 64))
         w2q = quantize("w2", w2_dealt, H)
 
         def first_layer(name, wq):
@@ -154,7 +162,7 @@ def tile_picked_hub_relu_lo_kernel(tc, xT, w1, w2, w3, offs, src, dst, out_0, ou
         y = first_layer("y", w1q)
         e = first_layer("e", w2q)
         w3_dealt = sbuf([P, PACK * H], BF16, "w3_dealt", tag="w_dealt")
-        nc.scalar.copy(*dealt_views(w3_dealt, w3_raw, 0, P))
+        nc.scalar.activation(*dealt_views(w3_dealt, w3_raw, 0, P), COPY)
 
         def gather_sources(into, ts, first, count):
             for n, t in enumerate(ts):
@@ -165,7 +173,7 @@ def tile_picked_hub_relu_lo_kernel(tc, xT, w1, w2, w3, offs, src, dst, out_0, ou
 
         def relu_views(z_bf, z, first, count):
             return (
-                z_bf[:].rearrange("p (c i t) -> p c t i", i=4, t=PACK),
+                z_bf.rearrange("p (c i t) -> p c t i", i=4, t=PACK),
                 z[:, :, first : first + count].rearrange("p t (c i) -> p c t i", i=4),
             )
 
@@ -174,79 +182,88 @@ def tile_picked_hub_relu_lo_kernel(tc, xT, w1, w2, w3, offs, src, dst, out_0, ou
         out_scale_rows = out_2.rearrange("z q c -> (z q) c").bitcast(I32)
         out_scales = sbuf([P, S], U8, "out_scales")
 
-        def second_layer(name, zq, first, count, rounded, round_on_vector=False, queue=nc.sync):
-            result = sbuf([P, PACK, count], F32, name + "_result")
-            for c in range(0, count, OUT_BLOCK):
-                bank = psum.tile([P, PACK, OUT_BLOCK], F32, name="second_bank")
-                for t in range(PACK):
-                    product(bank[:, t, :], w3q, t, zq, slice(c, c + OUT_BLOCK))
-                to = rounded[:, PACK * c : PACK * (c + OUT_BLOCK)].rearrange("p (c i t) -> p c t i", i=4, t=PACK)
-                of = bank[:].rearrange("p t (c i) -> p c t i", i=4)
-                if round_on_vector:
-                    nc.vector.tensor_copy(to, of)
-                else:
-                    nc.scalar.copy(to, of)
-                nc.scalar.copy(result[:, :, c : c + OUT_BLOCK], bank[:])
-            queue.dma_start(out=out_rows[:, :, first : first + count], in_=result[:])
+        def second_layer(zq, c, result, rounded):
+            bank = psum.tile([P, PACK, OUT_BLOCK], F32, name="second_bank")
+            for t in range(PACK):
+                product(bank[:, t, :], w3q, t, zq, slice(c, c + OUT_BLOCK))
+            nc.scalar.copy(
+                rounded.rearrange("p (c i t) -> p c t i", i=4, t=PACK),
+                bank[:].rearrange("p t (c i) -> p c t i", i=4),
+            )
+            nc.scalar.copy(result, bank[:])
+
+        def second_layer_block(name, zq, first, rounded, between=None):
+            result = sbuf([P, PACK, 256], F32, name + "_result")
+            second_layer(zq, 0, result[:, :, 0:128], rounded[:, 0:512])
+            if between:
+                between()
+            second_layer(zq, 128, result[:, :, 128:256], rounded[:, 512:1024])
+            nc.sync.dma_start(out=out_rows[:, :, first : first + 256], in_=result[:])
 
         def quantize_out(codes, rounded, first, count):
             cols = slice(first, first + count)
             nc.vector.quantize_mx(out=codes[:].bitcast(FP8X4), scales=out_scales[:, cols], in_=rounded[:])
             nc.sync.dma_start(out=out_words[:, cols], in_=codes[:].bitcast(I32))
 
-        g_a = sbuf([P, 3, 512], F32, "g_a")
-        gather_sources(g_a, range(3), 0, 512)
-        g03 = sbuf([P, 1, 256], F32, "g03", tag="A")
-        g13 = sbuf([P, 1, 256], F32, "g13")
-        gather_sources(g03, (3,), 0, 256)
-        gather_sources(g13, (3,), 256, 256)
-        z0 = sbuf([P, PACK, 256], F32, "z0")
-        for t in range(PACK):
-            add_targets(z0, t, g_a[:, t, 0:256] if t < 3 else g03[:, 0, :], 0, 256)
-        z1 = sbuf([P, PACK, 256], F32, "z1", tag="A")
-        for t in range(PACK):
-            add_targets(z1, t, g_a[:, t, 256:512] if t < 3 else g13[:, 0, :], 256, 256)
+        g_a = placed([P, PACK, 512], F32, "g_a", 8192)
+        gather_sources(g_a, range(PACK), 0, 512)
+        z_a = sbuf([P, PACK, 512], F32, "z_a")
+        for t in range(3):
+            add_targets(z_a, t, g_a[:, t, :], 0, 512)
+        for first in (0, 256):
+            add_targets(z_a[:, :, first : first + 256], 3, g_a[:, 3, first : first + 256], first, 256)
         w3q = quantize("w3", w3_dealt, H)
-        zb0 = sbuf([P, 1024], BF16, "zb0", tag="B")
+        zb0 = placed([P, 1024], BF16, "zb0", 6144)
         zb1 = placed([P, 1024], BF16, "zb1", 3072)
-        nc.scalar.activation(*relu_views(zb0, z0, 0, 256), RELU)
-        nc.scalar.activation(*relu_views(zb1, z1, 0, 256), RELU)
-        zq0 = quantize("z0", zb0, 256)
-        g2a = sbuf([P, 2, 256], F32, "g2a", tag="B")
-        gather_sources(g2a, (0, 1), 512, 256)
+        nc.scalar.activation(*relu_views(zb0[:], z_a, 0, 256), RELU)
+        nc.scalar.activation(*relu_views(zb1[:], z_a, 256, 256), RELU)
+        g2a = placed([P, 1, 256], F32, "g2a", 8192)
+        gather_sources(g2a, (0,), 512, 256)
+        zq0 = quantize("z0", zb0, 256, tag="w_dealt")
+        g2b = placed([P, 2, 256], F32, "g2b", 6144)
+        gather_sources(g2b, (1, 2), 512, 256)
         zq1 = quantize("z1", zb1, 256)
-        g2b = placed([P, 2, 256], F32, "g2b", 4096)
-        gather_sources(g2b, (2, 3), 512, 256)
+        g2c = placed([P, 1, 256], F32, "g2c", 4096)
+        gather_sources(g2c, (3,), 512, 256)
         ob01 = sbuf([P, PACK * 512], BF16, "ob01")
-        second_layer("o0", zq0, 0, 256, ob01[:, 0:1024])
-        second_layer("o1", zq1, 256, 256, ob01[:, 1024:2048])
+        second_layer_block("o0", zq0, 0, ob01[:, 0:1024])
+        second_layer_block("o1", zq1, 256, ob01[:, 1024:2048])
         z2 = placed([P, PACK, 256], F32, "z2", 0)
-        for t in range(PACK):
-            add_targets(z2, t, (g2a, g2b)[t // 2][:, t % 2, :], 512, 256)
-        zb2 = placed([P, 1024], BF16, "zb2", 11264)
-        nc.scalar.activation(*relu_views(zb2, z2, 0, 256), RELU)
-        g3a = placed([P, 2, 256], F32, "g3a", 4096)
-        gather_sources(g3a, (0, 1), 768, 256)
+        for t, fetched in enumerate((g2a[:, 0, :], g2b[:, 0, :], g2b[:, 1, :], g2c[:, 0, :])):
+            add_targets(z2, t, fetched, 512, 256)
+        zb2 = placed([P, 1024], BF16, "zb2", 20480)
+        nc.scalar.activation(*relu_views(zb2[:], z2, 0, 256), RELU)
+        g3a = placed([P, 3, 256], F32, "g3a", 4096)
+        gather_sources(g3a, (0, 1, 2), 768, 256)
         zq2 = quantize("z2", zb2, 256)
-        g3b = placed([P, 2, 256], F32, "g3b", 12288)
-        gather_sources(g3b, (2, 3), 768, 256)
+        g3b = placed([P, 1, 256], F32, "g3b", 20736)
+        gather_sources(g3b, (3,), 768, 256)
+        g3 = (g3a[:, 0, :], g3a[:, 1, :], g3a[:, 2, :], g3b[:, 0, :])
+        z3a = placed([P, PACK, 128], F32, "z3a", 18688)
+        for t in range(PACK):
+            add_targets(z3a, t, g3[t][:, 0:128], 768, 128)
+        z3b_flat = placed([P, PACK * 128], F32, "z3b", 21760)
+        z3b = z3b_flat[:].rearrange("p (t n) -> p t n", t=PACK)
+        zb3a = z3b_flat[:, 256:512].bitcast(BF16)
+        for t in (0, 1):
+            nc.vector.tensor_tensor(z3b_flat[:, 128 * t : 128 * (t + 1)], e[t][:].indirect(entries(dst_t, 896, 128)), g3[t][:, 128:256], ADD)
         ob2 = sbuf([P, PACK * 256], BF16, "ob2")
-        second_layer("o2", zq2, 512, 256, ob2)
-        z3 = placed([P, PACK, 256], F32, "z3", 8192)
-        zb3 = []
-        for n in range(2):
-            for t in range(PACK):
-                cols = slice(128 * n, 128 * (n + 1))
-                add_targets(z3[:, :, cols], t, (g3a, g3b)[t // 2][:, t % 2, cols], 768 + 128 * n, 128)
-            zb3.append(sbuf([P, 512], BF16, "zb3_%d" % n))
-            nc.scalar.activation(*relu_views(zb3[n], z3, 128 * n, 128), RELU)
-        zq3a = quantize("z3a", zb3[0], 128)
-        quantize_out(placed([P, 512], U32, "codes01", 4096), ob01, 0, 512)
-        zq3b = quantize("z3b", zb3[1], 128)
-        quantize_out(placed([P, 256], U32, "codes2", 12288), ob2, 512, 256)
+        second_layer_block("o2", zq2, 512, ob2, lambda: nc.scalar.activation(*relu_views(zb3a, z3a, 0, 128), RELU))
+        zq3a = quantize("z3a", zb3a, 128)
+        for t in (2, 3):
+            add_targets(z3b, t, g3[t][:, 128:256], 896, 128)
+        zb3b = placed([P, 512], BF16, "zb3b", 24576)
+        to, of = relu_views(zb3b[:], z3b, 0, 128)
+        nc.vector.tensor_scalar_max(to, of, 0.0)
+        zq3b = quantize("z3b", zb3b, 128)
+        quantize_out(placed([P, 512], U32, "codes01", 23040), ob01, 0, 512)
+        quantize_out(placed([P, 256], U32, "codes2", 25088), ob2, 512, 256)
         ob3 = sbuf([P, PACK * 256], BF16, "ob3")
-        second_layer("o3a", zq3a, 768, 128, ob3[:, 0:512])
-        second_layer("o3b", zq3b, 896, 128, ob3[:, 512:1024], round_on_vector=True, queue=nc.scalar)
+        for n, zq in enumerate((zq3a, zq3b)):
+            result = sbuf([P, PACK, 128], F32, "o3_result%d" % n)
+            second_layer(zq, 0, result[:], ob3[:, 512 * n : 512 * (n + 1)])
+            queue = nc.scalar if n else nc.sync
+            queue.dma_start(out=out_rows[:, :, 768 + 128 * n : 896 + 128 * n], in_=result[:])
         quantize_out(sbuf([P, 256], U32, "codes3"), ob3, 768, 256)
         for q in range(4):
             queue = nc.sync if q < 2 else nc.scalar

@@ -17,9 +17,33 @@ RELU = mybir.ActivationFunctionType.Relu
 COPY = mybir.ActivationFunctionType.Copy
 
 P = 128
-PACK = 4
+SLOTS = 4
 HALF = 512
-OUT_BLOCK = 128
+BLOCK = 256
+PART = 128
+RUN = 4
+PSUM_RING = 4
+
+X_LOADS = ((0, 0, 1024, 1024), (0, 1024, 1024, 320), (1, 0, 1024, 1024), (1, 1024, 512, 0), (1, 1536, 512, 160))
+
+KIB = 1024
+AT_W3_ROWS = 0
+AT_RELU0 = 6 * KIB
+AT_RELU1 = 3 * KIB
+AT_SRC01 = 8 * KIB
+AT_SRC2_FIRST = 8 * KIB
+AT_SRC2_MIDDLE = 6 * KIB
+AT_SRC2_LAST = 4 * KIB
+AT_SUM2 = 0
+AT_SRC3_FIRST = 4 * KIB
+AT_RELU2 = 20 * KIB
+AT_SUM3A = 18 * KIB + 256
+AT_SRC3_LAST = 20 * KIB + 256
+AT_SUM3B = 21 * KIB + 256
+AT_RELU3B = 24 * KIB
+AT_CODES01 = 22 * KIB + 512
+AT_CODES2 = 24 * KIB + 512
+AT_Y = 28 * KIB
 
 
 def tile_picked_hub_relu_lo_kernel(tc, xT, w1, w2, w3, offs, src, dst, out_0, out_1, out_2):
@@ -28,7 +52,7 @@ def tile_picked_hub_relu_lo_kernel(tc, xT, w1, w2, w3, offs, src, dst, out_0, ou
         lists = ctx.enter_context(tc.tile_pool(name="lists", bufs=1))
         pool = ctx.enter_context(tc.tile_pool(name="pool", bufs=1))
         staged = ctx.enter_context(tc.tile_pool(name="staged", bufs=1))
-        psum = ctx.enter_context(tc.psum_pool(name="psum", bufs=4))
+        psum = ctx.enter_context(tc.psum_pool(name="psum", bufs=PSUM_RING))
 
         def sbuf(shape, dtype, name, tag=None):
             return pool.tile(shape, dtype, name=name, tag=tag or name, align_bytes=64)
@@ -49,222 +73,232 @@ def tile_picked_hub_relu_lo_kernel(tc, xT, w1, w2, w3, offs, src, dst, out_0, ou
             nc.vector.quantize_mx(
                 out=operand[0][:, cols].bitcast(FP8X4),
                 scales=operand[1][:, cols],
-                in_=values[:, PACK * first : PACK * (first + count)],
+                in_=values,
             )
 
         def quantize(name, values, width, tag=None):
             operand = mx_tiles(name, width, tag)
-            quantize_part(operand, values, 0, width)
+            quantize_part(operand, values[:], 0, width)
             return operand
 
-        def product(out, stationary, t, moving, cols):
-            m = slice(P * t, P * (t + 1))
+        def product(out, weights, t, moving, cols):
+            group = slice(P * t, P * (t + 1))
             nc.tensor.matmul_mx(
                 out=out,
-                lhsT=stationary[0][:, m].bitcast(FP8X4),
-                lhsT_scale=stationary[1][:, m],
+                lhsT=weights[0][:, group].bitcast(FP8X4),
+                lhsT_scale=weights[1][:, group],
                 rhs=moving[0][:, cols].bitcast(FP8X4),
                 rhs_scale=moving[1][:, cols],
                 start=True,
                 stop=True,
             )
 
-        x_rows = xT.rearrange("(p j) n -> p j n", j=PACK)
-        offs_t = lists.tile([P, S // 16], U16, name="offs_t")
-        src_t = lists.tile([P, S // 16], U16, name="src_t")
-        dst_t = lists.tile([P, S // 16], U16, name="dst_t")
-        x_chunks = [(0, 0, 1024, 1024), (0, 1024, 1024, 320), (1, 0, 1024, 1024), (1, 1024, 512, 0), (1, 1536, 512, 160)]
-        raw = []
-        for n, (u, first, width, on_scalar) in enumerate(x_chunks):
-            chunk = sbuf([P, 2, width], F32, "x_raw%d" % n)
-            nc.sync.dma_start(out=chunk[:], in_=x_rows[:, 2 * u : 2 * u + 2, first : first + width])
-            raw.append(chunk)
+        def interleaving(words, slots):
+            return (
+                words.rearrange("p (c i t) -> p c t i", i=RUN, t=SLOTS),
+                slots.rearrange("p t (c i) -> p c t i", i=RUN),
+            )
+
+        x_rows = xT.rearrange("(p t) n -> p t n", t=SLOTS)
+        offs_tile = lists.tile([P, S // 16], U16, name="offs_tile")
+        src_tile = lists.tile([P, S // 16], U16, name="src_tile")
+        dst_tile = lists.tile([P, S // 16], U16, name="dst_tile")
+        x_loaded = []
+        for n, (u, first, width, on_scalar) in enumerate(X_LOADS):
+            piece = sbuf([P, 2, width], F32, "x_loaded%d" % n)
+            nc.sync.dma_start(out=piece[:], in_=x_rows[:, 2 * u : 2 * u + 2, first : first + width])
+            x_loaded.append(piece)
             if n == 0:
-                nc.sync.dma_start(offs_t[:], offs)
-        w1_rows = w1.rearrange("(p j) c -> p j c", j=PACK)
-        w1_raw = []
-        for n in range(2):
-            rows = sbuf([P, PACK, H // 2], F32, "w1_raw%d" % n)
-            nc.sync.dma_start(out=rows[:], in_=w1_rows[:, :, H // 2 * n : H // 2 * (n + 1)])
-            w1_raw.append(rows)
-        nc.sync.dma_start(src_t[:], src)
-        w2_raw = sbuf([P, PACK, H], F32, "w2_raw")
-        nc.sync.dma_start(out=w2_raw[:], in_=w2.rearrange("(p j) c -> p j c", j=PACK))
-        nc.sync.dma_start(dst_t[:], dst)
-        w3_raw = placed([P, PACK, H], F32, "w3_raw", 0)
-        w3_rows = w3.rearrange("(g t b) c -> b g t c", t=PACK, b=2)
+                nc.sync.dma_start(offs_tile[:], offs)
+
+        def load_halves(w, halves):
+            rows = w.rearrange("(p j) c -> p j c", j=SLOTS)
+            for n, half in enumerate(halves):
+                nc.sync.dma_start(out=half, in_=rows[:, :, H // 2 * n : H // 2 * (n + 1)])
+
+        w1_halves = [sbuf([P, SLOTS, H // 2], F32, "w1_half%d" % n)[:] for n in range(2)]
+        load_halves(w1, w1_halves)
+        nc.sync.dma_start(src_tile[:], src)
+        w2_halves = [
+            placed([P, SLOTS, S], F32, "w2_half0", AT_Y)[:, :, 0 : H // 2],
+            sbuf([P, SLOTS, H // 2], F32, "w2_half1")[:],
+        ]
+        load_halves(w2, w2_halves)
+        nc.sync.dma_start(dst_tile[:], dst)
+        w3_rows = placed([P, SLOTS, H], F32, "w3_rows", AT_W3_ROWS)
+        w3_by_b = w3.rearrange("(g t b) c -> b g t c", t=SLOTS, b=2)
         for b in range(2):
-            nc.sync.dma_start(out=w3_raw[b::2], in_=w3_rows[b])
+            nc.sync.dma_start(out=w3_rows[b::2], in_=w3_by_b[b])
 
         pairs = [sbuf([P, 2 * T], BF16, "pairs%d" % u) for u in range(2)]
-        picked = [sbuf([P, PACK * HALF], BF16, "picked%d" % h) for h in range(2)]
+        picked = [sbuf([P, SLOTS * HALF], BF16, "picked%d" % h) for h in range(2)]
 
         def gather_x(u, h):
             nc.vector.tensor_copy(
                 picked[h][:].bitcast(U32)[:, u::2],
-                pairs[u][:].bitcast(U32).indirect(entries(offs_t, HALF * h, HALF)),
+                pairs[u][:].bitcast(U32).indirect(entries(offs_tile, HALF * h, HALF)),
             )
 
-        def pair_views(n, a, b):
-            u, first = x_chunks[n][:2]
+        def pairing(n, a, b):
+            u, first = X_LOADS[n][:2]
             return (
-                pairs[u][:, 2 * (first + a) : 2 * (first + b)].rearrange("p (c i e) -> p c e i", i=4, e=2),
-                raw[n][:, :, a:b].rearrange("p e (c i) -> p c e i", i=4),
+                pairs[u][:, 2 * (first + a) : 2 * (first + b)].rearrange("p (c i e) -> p c e i", i=RUN, e=2),
+                x_loaded[n][:, :, a:b].rearrange("p e (c i) -> p c e i", i=RUN),
             )
 
-        for n, (u, first, width, on_scalar) in enumerate(x_chunks):
+        for n, (u, first, width, on_scalar) in enumerate(X_LOADS):
             if on_scalar:
-                nc.scalar.copy(*pair_views(n, 0, on_scalar))
+                nc.scalar.copy(*pairing(n, 0, on_scalar))
             if on_scalar < width:
-                nc.vector.tensor_copy(*pair_views(n, on_scalar, width))
-            if (u, first + width) == (0, T):
+                nc.vector.tensor_copy(*pairing(n, on_scalar, width))
+            if u == 0 and first + width == T:
                 gather_x(0, 0)
                 gather_x(0, 1)
 
-        def dealt_views(dealt, rows, m0, m1):
+        def dealing(dealt, halves, n, t0, t1):
+            groups = P // 2
             return (
-                dealt[:].rearrange("p (t m j) -> p m j t", t=PACK, j=PACK)[:, m0:m1],
-                rows[:].rearrange("p j (m t) -> p m j t", t=PACK),
+                dealt[:].rearrange("p (t g b j) -> p g t j b", g=groups, b=2, j=SLOTS)[:, groups // 2 * n : groups // 2 * (n + 1)],
+                halves[n].rearrange("p j (g t b) -> p g t j b", t=SLOTS, b=2)[:, :, t0:t1],
             )
 
-        def hidden_views(dealt, rows, g0, g1):
-            return (
-                dealt[:].rearrange("p (t g b j) -> p g t j b", t=PACK, b=2, j=PACK)[:, g0:g1],
-                rows[:].rearrange("p j (g t b) -> p g t j b", t=PACK, b=2),
-            )
-
-        w1_dealt = sbuf([P, PACK * H], BF16, "w1_dealt", tag="w_dealt")
+        w1_first = sbuf([P, SLOTS * P], BF16, "w1_first")
+        w1_rest = sbuf([P, SLOTS * 3 * P], BF16, "w1_rest")
         for n in range(2):
-            nc.scalar.copy(*hidden_views(w1_dealt, w1_raw[n], 32 * n, 32 * (n + 1)))
+            nc.scalar.copy(*dealing(w1_first, w1_halves, n, 0, 1))
+            nc.scalar.copy(*dealing(w1_rest, w1_halves, n, 1, SLOTS))
+        w2_dealt = sbuf([P, SLOTS * H], BF16, "w2_dealt", tag="dealt")
+        nc.scalar.copy(*dealing(w2_dealt, w2_halves, 0, 0, SLOTS))
         gather_x(1, 0)
         gather_x(1, 1)
         xq = [quantize("x0", picked[0], HALF)]
         w1q = mx_tiles("w1", H)
-        quantize_part(w1q, w1_dealt, 0, 128)
-        xq.append(quantize("x1", picked[1], HALF))
-        quantize_part(w1q, w1_dealt, 128, 128)
-        quantize_part(w1q, w1_dealt, 256, 256)
-        w2_dealt = sbuf([P, PACK * H], BF16, "w2_dealt", tag="w_dealt")
-        nc.vector.tensor_copy(*hidden_views(w2_dealt, w2_raw, 0, 64))
+        quantize_part(w1q, w1_first[:], 0, P)
+        xq.append(quantize("x1", picked[1], HALF, tag="w1_first"))
+        quantize_part(w1q, w1_rest[:, 0 : SLOTS * P], P, P)
+        quantize_part(w1q, w1_rest[:, SLOTS * P :], 2 * P, 2 * P)
+        nc.vector.tensor_copy(*dealing(w2_dealt, w2_halves, 1, 0, SLOTS))
         w2q = quantize("w2", w2_dealt, H)
 
-        def first_layer(name, wq):
-            rows = []
-            for t in range(PACK):
-                row = sbuf([P, S], F32, "%s%d" % (name, t))
+        def first_layer(rows, wq):
+            for t in range(SLOTS):
                 for h in range(2):
                     bank = psum.tile([P, HALF], F32, name="first_bank")
                     product(bank[:], wq, t, xq[h], slice(0, HALF))
-                    nc.scalar.copy(row[:, HALF * h : HALF * (h + 1)], bank[:])
-                rows.append(row)
-            return rows
+                    nc.scalar.copy(rows[t][:, HALF * h : HALF * (h + 1)], bank[:])
 
-        y = first_layer("y", w1q)
-        e = first_layer("e", w2q)
-        w3_dealt = sbuf([P, PACK * H], BF16, "w3_dealt", tag="w_dealt")
-        nc.scalar.activation(*dealt_views(w3_dealt, w3_raw, 0, P), COPY)
+        y = [placed([P, S], F32, "y%d" % t, AT_Y + 4 * S * t) for t in range(SLOTS)]
+        first_layer(y, w1q)
+        e = [sbuf([P, S], F32, "e%d" % t) for t in range(SLOTS)]
+        first_layer(e, w2q)
 
-        def gather_sources(into, ts, first, count):
-            for n, t in enumerate(ts):
-                nc.vector.tensor_copy(into[:, n, :], y[t][:].indirect(entries(src_t, first, count)))
+        w3_dealt = sbuf([P, SLOTS * H], BF16, "w3_dealt", tag="dealt")
+        nc.scalar.activation(
+            w3_dealt[:].rearrange("p (t c j) -> p c j t", t=SLOTS, j=SLOTS),
+            w3_rows[:].rearrange("p j (c t) -> p c j t", t=SLOTS),
+            COPY,
+        )
 
-        def add_targets(into, t, fetched, first, count):
-            nc.vector.tensor_tensor(into[:, t, :], e[t][:].indirect(entries(dst_t, first, count)), fetched, ADD)
+        def gather_sources(into, slots, first, count):
+            for n, t in enumerate(slots):
+                nc.vector.tensor_copy(into[:, n, :], y[t][:].indirect(entries(src_tile, first, count)))
 
-        def relu_views(z_bf, z, first, count):
-            return (
-                z_bf.rearrange("p (c i t) -> p c t i", i=4, t=PACK),
-                z[:, :, first : first + count].rearrange("p t (c i) -> p c t i", i=4),
-            )
+        def add_targets(total, t, sources, first, count):
+            nc.vector.tensor_tensor(total, e[t][:].indirect(entries(dst_tile, first, count)), sources, ADD)
 
-        out_rows = out_0.rearrange("(p t) r -> p t r", t=PACK)
+        out_rows = out_0.rearrange("(p t) r -> p t r", t=SLOTS)
         out_words = out_1.rearrange("z p c r -> (z p) (c r)").bitcast(I32)
         out_scale_rows = out_2.rearrange("z q c -> (z q) c").bitcast(I32)
         out_scales = sbuf([P, S], U8, "out_scales")
 
-        def second_layer(zq, c, result, rounded):
-            bank = psum.tile([P, PACK, OUT_BLOCK], F32, name="second_bank")
-            for t in range(PACK):
-                product(bank[:, t, :], w3q, t, zq, slice(c, c + OUT_BLOCK))
-            nc.scalar.copy(
-                rounded.rearrange("p (c i t) -> p c t i", i=4, t=PACK),
-                bank[:].rearrange("p t (c i) -> p c t i", i=4),
-            )
+        def second_layer(zq, first, result, rounded):
+            bank = psum.tile([P, SLOTS, PART], F32, name="second_bank")
+            for t in range(SLOTS):
+                product(bank[:, t, :], w3q, t, zq, slice(first, first + PART))
+            nc.scalar.copy(*interleaving(rounded, bank[:]))
             nc.scalar.copy(result, bank[:])
 
-        def second_layer_block(name, zq, first, rounded, between=None):
-            result = sbuf([P, PACK, 256], F32, name + "_result")
-            second_layer(zq, 0, result[:, :, 0:128], rounded[:, 0:512])
-            if between:
-                between()
-            second_layer(zq, 128, result[:, :, 128:256], rounded[:, 512:1024])
-            nc.sync.dma_start(out=out_rows[:, :, first : first + 256], in_=result[:])
+        def second_layer_part(zq, n, result, rounded):
+            second_layer(zq, PART * n, result[:, :, PART * n : PART * (n + 1)], rounded[:, SLOTS * PART * n : SLOTS * PART * (n + 1)])
+
+        def store_result(result, first, count, queue):
+            queue.dma_start(out=out_rows[:, :, first : first + count], in_=result[:])
 
         def quantize_out(codes, rounded, first, count):
             cols = slice(first, first + count)
             nc.vector.quantize_mx(out=codes[:].bitcast(FP8X4), scales=out_scales[:, cols], in_=rounded[:])
             nc.sync.dma_start(out=out_words[:, cols], in_=codes[:].bitcast(I32))
 
-        g_a = placed([P, PACK, 512], F32, "g_a", 8192)
-        gather_sources(g_a, range(PACK), 0, 512)
-        z_a = sbuf([P, PACK, 512], F32, "z_a")
-        for t in range(3):
-            add_targets(z_a, t, g_a[:, t, :], 0, 512)
-        for first in (0, 256):
-            add_targets(z_a[:, :, first : first + 256], 3, g_a[:, 3, first : first + 256], first, 256)
+        src01 = placed([P, SLOTS, 2 * BLOCK], F32, "src01", AT_SRC01)
+        gather_sources(src01, range(SLOTS), 0, 2 * BLOCK)
+        sum01 = sbuf([P, SLOTS, 2 * BLOCK], F32, "sum01")
+        last = SLOTS - 1
+        for t in range(last):
+            add_targets(sum01[:, t, :], t, src01[:, t, :], 0, 2 * BLOCK)
+        for first in (0, BLOCK):
+            cols = slice(first, first + BLOCK)
+            add_targets(sum01[:, last, cols], last, src01[:, last, cols], first, BLOCK)
         w3q = quantize("w3", w3_dealt, H)
-        zb0 = placed([P, 1024], BF16, "zb0", 6144)
-        zb1 = placed([P, 1024], BF16, "zb1", 3072)
-        nc.scalar.activation(*relu_views(zb0[:], z_a, 0, 256), RELU)
-        nc.scalar.activation(*relu_views(zb1[:], z_a, 256, 256), RELU)
-        g2a = placed([P, 1, 256], F32, "g2a", 8192)
-        gather_sources(g2a, (0,), 512, 256)
-        zq0 = quantize("z0", zb0, 256, tag="w_dealt")
-        g2b = placed([P, 2, 256], F32, "g2b", 6144)
-        gather_sources(g2b, (1, 2), 512, 256)
-        zq1 = quantize("z1", zb1, 256)
-        g2c = placed([P, 1, 256], F32, "g2c", 4096)
-        gather_sources(g2c, (3,), 512, 256)
-        ob01 = sbuf([P, PACK * 512], BF16, "ob01")
-        second_layer_block("o0", zq0, 0, ob01[:, 0:1024])
-        second_layer_block("o1", zq1, 256, ob01[:, 1024:2048])
-        z2 = placed([P, PACK, 256], F32, "z2", 0)
-        for t, fetched in enumerate((g2a[:, 0, :], g2b[:, 0, :], g2b[:, 1, :], g2c[:, 0, :])):
-            add_targets(z2, t, fetched, 512, 256)
-        zb2 = placed([P, 1024], BF16, "zb2", 20480)
-        nc.scalar.activation(*relu_views(zb2[:], z2, 0, 256), RELU)
-        g3a = placed([P, 3, 256], F32, "g3a", 4096)
-        gather_sources(g3a, (0, 1, 2), 768, 256)
-        zq2 = quantize("z2", zb2, 256)
-        g3b = placed([P, 1, 256], F32, "g3b", 20736)
-        gather_sources(g3b, (3,), 768, 256)
-        g3 = (g3a[:, 0, :], g3a[:, 1, :], g3a[:, 2, :], g3b[:, 0, :])
-        z3a = placed([P, PACK, 128], F32, "z3a", 18688)
-        for t in range(PACK):
-            add_targets(z3a, t, g3[t][:, 0:128], 768, 128)
-        z3b_flat = placed([P, PACK * 128], F32, "z3b", 21760)
-        z3b = z3b_flat[:].rearrange("p (t n) -> p t n", t=PACK)
-        zb3a = z3b_flat[:, 256:512].bitcast(BF16)
+        relu0 = placed([P, SLOTS * BLOCK], BF16, "relu0", AT_RELU0)
+        relu1 = placed([P, SLOTS * BLOCK], BF16, "relu1", AT_RELU1)
+        nc.scalar.activation(*interleaving(relu0[:], sum01[:, :, 0:BLOCK]), RELU)
+        nc.scalar.activation(*interleaving(relu1[:], sum01[:, :, BLOCK:]), RELU)
+
+        src2_first = placed([P, 1, BLOCK], F32, "src2_first", AT_SRC2_FIRST)
+        gather_sources(src2_first, (0,), 2 * BLOCK, BLOCK)
+        z0q = quantize("z0", relu0, BLOCK, tag="dealt")
+        src2_middle = placed([P, 2, BLOCK], F32, "src2_middle", AT_SRC2_MIDDLE)
+        gather_sources(src2_middle, (1, 2), 2 * BLOCK, BLOCK)
+        z1q = quantize("z1", relu1, BLOCK)
+        src2_last = placed([P, 1, BLOCK], F32, "src2_last", AT_SRC2_LAST)
+        gather_sources(src2_last, (3,), 2 * BLOCK, BLOCK)
+        rounded01 = sbuf([P, SLOTS * 2 * BLOCK], BF16, "rounded01")
+        for block, zq in enumerate((z0q, z1q)):
+            result = sbuf([P, SLOTS, BLOCK], F32, "result%d" % block)
+            for n in range(2):
+                second_layer_part(zq, n, result, rounded01[:, SLOTS * BLOCK * block : SLOTS * BLOCK * (block + 1)])
+            store_result(result, BLOCK * block, BLOCK, nc.sync)
+        sum2 = placed([P, SLOTS, BLOCK], F32, "sum2", AT_SUM2)
+        src2 = (src2_first[:, 0, :], src2_middle[:, 0, :], src2_middle[:, 1, :], src2_last[:, 0, :])
+        for t in range(SLOTS):
+            add_targets(sum2[:, t, :], t, src2[t], 2 * BLOCK, BLOCK)
+        relu2 = placed([P, SLOTS * BLOCK], BF16, "relu2", AT_RELU2)
+        nc.scalar.activation(*interleaving(relu2[:], sum2[:]), RELU)
+
+        first_a, first_b = 3 * BLOCK, 3 * BLOCK + PART
+        src3_first = placed([P, 3, BLOCK], F32, "src3_first", AT_SRC3_FIRST)
+        gather_sources(src3_first, (0, 1, 2), first_a, BLOCK)
+        z2q = quantize("z2", relu2, BLOCK)
+        src3_last = placed([P, 1, BLOCK], F32, "src3_last", AT_SRC3_LAST)
+        gather_sources(src3_last, (3,), first_a, BLOCK)
+        src3 = (src3_first[:, 0, :], src3_first[:, 1, :], src3_first[:, 2, :], src3_last[:, 0, :])
+        sum3a = placed([P, SLOTS, PART], F32, "sum3a", AT_SUM3A)
+        for t in range(SLOTS):
+            add_targets(sum3a[:, t, :], t, src3[t][:, 0:PART], first_a, PART)
+        sum3b = placed([P, SLOTS * PART], F32, "sum3b", AT_SUM3B)
+        relu3a = sum3b[:, 2 * PART :].bitcast(BF16)
         for t in (0, 1):
-            nc.vector.tensor_tensor(z3b_flat[:, 128 * t : 128 * (t + 1)], e[t][:].indirect(entries(dst_t, 896, 128)), g3[t][:, 128:256], ADD)
-        ob2 = sbuf([P, PACK * 256], BF16, "ob2")
-        second_layer_block("o2", zq2, 512, ob2, lambda: nc.scalar.activation(*relu_views(zb3a, z3a, 0, 128), RELU))
-        zq3a = quantize("z3a", zb3a, 128)
+            add_targets(sum3b[:, PART * t : PART * (t + 1)], t, src3[t][:, PART:], first_b, PART)
+        rounded2 = sbuf([P, SLOTS * BLOCK], BF16, "rounded2")
+        result2 = sbuf([P, SLOTS, BLOCK], F32, "result2")
+        second_layer_part(z2q, 0, result2, rounded2)
+        nc.scalar.activation(*interleaving(relu3a, sum3a[:]), RELU)
+        second_layer_part(z2q, 1, result2, rounded2)
+        store_result(result2, 2 * BLOCK, BLOCK, nc.sync)
+        z3aq = quantize("z3a", relu3a, PART)
         for t in (2, 3):
-            add_targets(z3b, t, g3[t][:, 128:256], 896, 128)
-        zb3b = placed([P, 512], BF16, "zb3b", 24576)
-        to, of = relu_views(zb3b[:], z3b, 0, 128)
-        nc.vector.tensor_scalar_max(to, of, 0.0)
-        zq3b = quantize("z3b", zb3b, 128)
-        quantize_out(placed([P, 512], U32, "codes01", 23040), ob01, 0, 512)
-        quantize_out(placed([P, 256], U32, "codes2", 25088), ob2, 512, 256)
-        ob3 = sbuf([P, PACK * 256], BF16, "ob3")
-        for n, zq in enumerate((zq3a, zq3b)):
-            result = sbuf([P, PACK, 128], F32, "o3_result%d" % n)
-            second_layer(zq, 0, result[:], ob3[:, 512 * n : 512 * (n + 1)])
-            queue = nc.scalar if n else nc.sync
-            queue.dma_start(out=out_rows[:, :, 768 + 128 * n : 896 + 128 * n], in_=result[:])
-        quantize_out(sbuf([P, 256], U32, "codes3"), ob3, 768, 256)
-        for q in range(4):
-            queue = nc.sync if q < 2 else nc.scalar
+            add_targets(sum3b[:, PART * t : PART * (t + 1)], t, src3[t][:, PART:], first_b, PART)
+        relu3b = placed([P, SLOTS * PART], BF16, "relu3b", AT_RELU3B)
+        nc.vector.tensor_scalar_max(*interleaving(relu3b[:], sum3b[:].rearrange("p (t n) -> p t n", t=SLOTS)), 0.0)
+        z3bq = quantize("z3b", relu3b, PART)
+
+        quantize_out(placed([P, 2 * BLOCK], U32, "codes01", AT_CODES01), rounded01, 0, 2 * BLOCK)
+        quantize_out(placed([P, BLOCK], U32, "codes2", AT_CODES2), rounded2, 2 * BLOCK, BLOCK)
+        rounded3 = sbuf([P, SLOTS * BLOCK], BF16, "rounded3")
+        for n, (zq, first, queue) in enumerate(((z3aq, first_a, nc.sync), (z3bq, first_b, nc.scalar))):
+            result = sbuf([P, SLOTS, PART], F32, "result3_%d" % n)
+            second_layer(zq, 0, result[:], rounded3[:, SLOTS * PART * n : SLOTS * PART * (n + 1)])
+            store_result(result, first, PART, queue)
+        quantize_out(sbuf([P, BLOCK], U32, "codes3"), rounded3, first_a, BLOCK)
+        for q, queue in enumerate((nc.sync, nc.sync, nc.scalar, nc.scalar)):
             queue.dma_start(out=out_scale_rows[4 * q : 4 * q + 4, :], in_=out_scales[32 * q : 32 * q + 4, :].bitcast(I32))

@@ -41,8 +41,7 @@ AT_SUM3A = 18 * KIB + 256
 AT_SRC3_LAST = 20 * KIB + 256
 AT_SUM3B = 21 * KIB + 256
 AT_RELU3B = 24 * KIB
-AT_CODES01 = 22 * KIB + 512
-AT_CODES2 = 24 * KIB + 512
+AT_CODES012 = 24 * KIB
 AT_Y = 28 * KIB
 
 
@@ -225,9 +224,10 @@ def tile_picked_hub_relu_lo_kernel(tc, xT, w1, w2, w3, offs, src, dst, out_0, ou
             queue.dma_start(out=out_rows[:, :, first : first + count], in_=result[:])
 
         def quantize_out(codes, rounded, first, count):
-            cols = slice(first, first + count)
-            nc.vector.quantize_mx(out=codes[:].bitcast(FP8X4), scales=out_scales[:, cols], in_=rounded[:])
-            nc.sync.dma_start(out=out_words[:, cols], in_=codes[:].bitcast(I32))
+            nc.vector.quantize_mx(out=codes.bitcast(FP8X4), scales=out_scales[:, first : first + count], in_=rounded[:])
+
+        def store_codes(codes, first, count):
+            nc.sync.dma_start(out=out_words[:, first : first + count], in_=codes[:].bitcast(I32))
 
         src01 = placed([P, SLOTS, 2 * BLOCK], F32, "src01", AT_SRC01)
         gather_sources(src01, range(SLOTS), 0, 2 * BLOCK)
@@ -292,13 +292,17 @@ def tile_picked_hub_relu_lo_kernel(tc, xT, w1, w2, w3, offs, src, dst, out_0, ou
         nc.vector.tensor_scalar_max(*interleaving(relu3b[:], sum3b[:].rearrange("p (t n) -> p t n", t=SLOTS)), 0.0)
         z3bq = quantize("z3b", relu3b, PART)
 
-        quantize_out(placed([P, 2 * BLOCK], U32, "codes01", AT_CODES01), rounded01, 0, 2 * BLOCK)
-        quantize_out(placed([P, BLOCK], U32, "codes2", AT_CODES2), rounded2, 2 * BLOCK, BLOCK)
+        codes012 = placed([P, 3 * BLOCK], U32, "codes012", AT_CODES012)
+        quantize_out(codes012[:, 0 : 2 * BLOCK], rounded01, 0, 2 * BLOCK)
+        quantize_out(codes012[:, 2 * BLOCK :], rounded2, 2 * BLOCK, BLOCK)
+        store_codes(codes012, 0, 3 * BLOCK)
         rounded3 = sbuf([P, SLOTS * BLOCK], BF16, "rounded3")
         for n, (zq, first, queue) in enumerate(((z3aq, first_a, nc.sync), (z3bq, first_b, nc.scalar))):
             result = sbuf([P, SLOTS, PART], F32, "result3_%d" % n)
             second_layer(zq, 0, result[:], rounded3[:, SLOTS * PART * n : SLOTS * PART * (n + 1)])
             store_result(result, first, PART, queue)
-        quantize_out(sbuf([P, BLOCK], U32, "codes3"), rounded3, first_a, BLOCK)
+        codes3 = sbuf([P, BLOCK], U32, "codes3")
+        quantize_out(codes3[:], rounded3, first_a, BLOCK)
+        store_codes(codes3, first_a, BLOCK)
         for q, queue in enumerate((nc.sync, nc.sync, nc.scalar, nc.scalar)):
             queue.dma_start(out=out_scale_rows[4 * q : 4 * q + 4, :], in_=out_scales[32 * q : 32 * q + 4, :].bitcast(I32))

from contextlib import ExitStack

import concourse.mybir as mybir

K, T, S, H = 512, 2048, 1024, 512
FLOPS = 3 * 2 * K * H * S

F32 = mybir.dt.float32
BF16 = mybir.dt.bfloat16
U32 = mybir.dt.uint32
I32 = mybir.dt.int32
U16 = mybir.dt.uint16
U8 = mybir.dt.uint8
FP8X4 = mybir.dt.float8_e4m3fn_x4
ADD = mybir.AluOpType.add
RELU = mybir.ActivationFunctionType.Relu
COPY = mybir.ActivationFunctionType.Copy

P = 128
SLOTS = 4
HALF = 512
BLOCK = 256
PART = 128
RUN = 4
PSUM_RING = 4

X_LOADS = ((0, 0, 1024, 1024), (0, 1024, 1024, 320), (1, 0, 1024, 1024), (1, 1024, 512, 0), (1, 1536, 512, 160))

KIB = 1024
AT_W3_ROWS = 0
AT_RELU0 = 6 * KIB
AT_RELU1 = 3 * KIB
AT_SRC01 = 8 * KIB
AT_SRC2_FIRST = 8 * KIB
AT_SRC2_MIDDLE = 6 * KIB
AT_SRC2_LAST = 4 * KIB
AT_SUM2 = 0
AT_SRC3_FIRST = 4 * KIB
AT_RELU2 = 20 * KIB
AT_SUM3A = 18 * KIB + 256
AT_SRC3_LAST = 20 * KIB + 256
AT_SUM3B = 21 * KIB + 256
AT_RELU3B = 24 * KIB
AT_CODES012 = 24 * KIB
AT_Y = 28 * KIB


def tile_picked_hub_relu_lo_kernel(tc, xT, w1, w2, w3, offs, src, dst, out_0, out_1, out_2):
    nc = tc.nc
    with ExitStack() as ctx:
        lists = ctx.enter_context(tc.tile_pool(name="lists", bufs=1))
        pool = ctx.enter_context(tc.tile_pool(name="pool", bufs=1))
        staged = ctx.enter_context(tc.tile_pool(name="staged", bufs=1))
        psum = ctx.enter_context(tc.psum_pool(name="psum", bufs=PSUM_RING))

        def sbuf(shape, dtype, name, tag=None):
            return pool.tile(shape, dtype, name=name, tag=tag or name, align_bytes=64)

        def placed(shape, dtype, name, offset):
            return staged.tile(shape, dtype, name=name, align_bytes=64, offset=offset)

        def entries(list_tile, first, count):
            return list_tile[:, first // 16 : (first + count) // 16]

        def mx_tiles(name, width, tag=None):
            codes = sbuf([P, width], U32, name + "_codes", tag=tag)
            scales = sbuf([P, width], U8, name + "_scales")
            return codes, scales

        def quantize_part(operand, values, first, count):
            cols = slice(first, first + count)
            nc.vector.quantize_mx(
                out=operand[0][:, cols].bitcast(FP8X4),
                scales=operand[1][:, cols],
                in_=values,
            )

        def quantize(name, values, width, tag=None):
            operand = mx_tiles(name, width, tag)
            quantize_part(operand, values[:], 0, width)
            return operand

        def product(out, weights, t, moving, cols):
            group = slice(P * t, P * (t + 1))
            nc.tensor.matmul_mx(
                out=out,
                lhsT=weights[0][:, group].bitcast(FP8X4),
                lhsT_scale=weights[1][:, group],
                rhs=moving[0][:, cols].bitcast(FP8X4),
                rhs_scale=moving[1][:, cols],
                start=True,
                stop=True,
            )

        def interleaving(words, slots):
            return (
                words.rearrange("p (c i t) -> p c t i", i=RUN, t=SLOTS),
                slots.rearrange("p t (c i) -> p c t i", i=RUN),
            )

        x_rows = xT.rearrange("(p t) n -> p t n", t=SLOTS)
        offs_tile = lists.tile([P, S // 16], U16, name="offs_tile")
        src_tile = lists.tile([P, S // 16], U16, name="src_tile")
        dst_tile = lists.tile([P, S // 16], U16, name="dst_tile")
        x_loaded = []
        for n, (u, first, width, on_scalar) in enumerate(X_LOADS):
            piece = sbuf([P, 2, width], F32, "x_loaded%d" % n)
            nc.sync.dma_start(out=piece[:], in_=x_rows[:, 2 * u : 2 * u + 2, first : first + width])
            x_loaded.append(piece)
            if n == 0:
                nc.sync.dma_start(offs_tile[:], offs)

        def load_halves(w, halves):
            rows = w.rearrange("(p j) c -> p j c", j=SLOTS)
            for n, half in enumerate(halves):
                nc.sync.dma_start(out=half, in_=rows[:, :, H // 2 * n : H // 2 * (n + 1)])

        w1_halves = [sbuf([P, SLOTS, H // 2], F32, "w1_half%d" % n)[:] for n in range(2)]
        load_halves(w1, w1_halves)
        nc.sync.dma_start(src_tile[:], src)
        w2_halves = [
            placed([P, SLOTS, S], F32, "w2_half0", AT_Y)[:, :, 0 : H // 2],
            sbuf([P, SLOTS, H // 2], F32, "w2_half1")[:],
        ]
        load_halves(w2, w2_halves)
        nc.sync.dma_start(dst_tile[:], dst)
        w3_rows = placed([P, SLOTS, H], F32, "w3_rows", AT_W3_ROWS)
        w3_by_b = w3.rearrange("(g t b) c -> b g t c", t=SLOTS, b=2)
        for b in range(2):
            nc.sync.dma_start(out=w3_rows[b::2], in_=w3_by_b[b])

        pairs = [sbuf([P, 2 * T], BF16, "pairs%d" % u) for u in range(2)]
        picked = [sbuf([P, SLOTS * HALF], BF16, "picked%d" % h) for h in range(2)]

        def gather_x(u, h):
            nc.vector.tensor_copy(
                picked[h][:].bitcast(U32)[:, u::2],
                pairs[u][:].bitcast(U32).indirect(entries(offs_tile, HALF * h, HALF)),
            )

        def pairing(n, a, b):
            u, first = X_LOADS[n][:2]
            return (
                pairs[u][:, 2 * (first + a) : 2 * (first + b)].rearrange("p (c i e) -> p c e i", i=RUN, e=2),
                x_loaded[n][:, :, a:b].rearrange("p e (c i) -> p c e i", i=RUN),
            )

        for n, (u, first, width, on_scalar) in enumerate(X_LOADS):
            if on_scalar:
                nc.scalar.copy(*pairing(n, 0, on_scalar))
            if on_scalar < width:
                nc.vector.tensor_copy(*pairing(n, on_scalar, width))
            if u == 0 and first + width == T:
                gather_x(0, 0)
                gather_x(0, 1)

        def dealing(dealt, halves, n, t0, t1):
            groups = P // 2
            return (
                dealt[:].rearrange("p (t g b j) -> p g t j b", g=groups, b=2, j=SLOTS)[:, groups // 2 * n : groups // 2 * (n + 1)],
                halves[n].rearrange("p j (g t b) -> p g t j b", t=SLOTS, b=2)[:, :, t0:t1],
            )

        w1_first = sbuf([P, SLOTS * P], BF16, "w1_first")
        w1_rest = sbuf([P, SLOTS * 3 * P], BF16, "w1_rest")
        for n in range(2):
            nc.scalar.copy(*dealing(w1_first, w1_halves, n, 0, 1))
            nc.scalar.copy(*dealing(w1_rest, w1_halves, n, 1, SLOTS))
        w2_dealt = sbuf([P, SLOTS * H], BF16, "w2_dealt", tag="dealt")
        nc.scalar.copy(*dealing(w2_dealt, w2_halves, 0, 0, SLOTS))
        gather_x(1, 0)
        gather_x(1, 1)
        xq = [quantize("x0", picked[0], HALF)]
        w1q = mx_tiles("w1", H)
        quantize_part(w1q, w1_first[:], 0, P)
        xq.append(quantize("x1", picked[1], HALF, tag="w1_first"))
        quantize_part(w1q, w1_rest[:, 0 : SLOTS * P], P, P)
        quantize_part(w1q, w1_rest[:, SLOTS * P :], 2 * P, 2 * P)
        nc.vector.tensor_copy(*dealing(w2_dealt, w2_halves, 1, 0, SLOTS))
        w2q = quantize("w2", w2_dealt, H)

        def first_layer(rows, wq):
            for t in range(SLOTS):
                for h in range(2):
                    bank = psum.tile([P, HALF], F32, name="first_bank")
                    product(bank[:], wq, t, xq[h], slice(0, HALF))
                    nc.scalar.copy(rows[t][:, HALF * h : HALF * (h + 1)], bank[:])

        y = [placed([P, S], F32, "y%d" % t, AT_Y + 4 * S * t) for t in range(SLOTS)]
        first_layer(y, w1q)
        e = [sbuf([P, S], F32, "e%d" % t) for t in range(SLOTS)]
        first_layer(e, w2q)

        w3_dealt = sbuf([P, SLOTS * H], BF16, "w3_dealt", tag="dealt")
        nc.scalar.activation(
            w3_dealt[:].rearrange("p (t c j) -> p c j t", t=SLOTS, j=SLOTS),
            w3_rows[:].rearrange("p j (c t) -> p c j t", t=SLOTS),
            COPY,
        )

        def gather_sources(into, slots, first, count):
            for n, t in enumerate(slots):
                nc.vector.tensor_copy(into[:, n, :], y[t][:].indirect(entries(src_tile, first, count)))

        def add_targets(total, t, sources, first, count):
            nc.vector.tensor_tensor(total, e[t][:].indirect(entries(dst_tile, first, count)), sources, ADD)

        out_rows = out_0.rearrange("(p t) r -> p t r", t=SLOTS)
        out_words = out_1.rearrange("z p c r -> (z p) (c r)").bitcast(I32)
        out_scale_rows = out_2.rearrange("z q c -> (z q) c").bitcast(I32)
        out_scales = sbuf([P, S], U8, "out_scales")

        def second_layer(zq, first, result, rounded):
            bank = psum.tile([P, SLOTS, PART], F32, name="second_bank")
            for t in range(SLOTS):
                product(bank[:, t, :], w3q, t, zq, slice(first, first + PART))
            nc.scalar.copy(*interleaving(rounded, bank[:]))
            nc.scalar.copy(result, bank[:])

        def second_layer_part(zq, n, result, rounded):
            second_layer(zq, PART * n, result[:, :, PART * n : PART * (n + 1)], rounded[:, SLOTS * PART * n : SLOTS * PART * (n + 1)])

        def store_result(result, first, count, queue):
            queue.dma_start(out=out_rows[:, :, first : first + count], in_=result[:])

        def quantize_out(codes, rounded, first, count):
            nc.vector.quantize_mx(out=codes.bitcast(FP8X4), scales=out_scales[:, first : first + count], in_=rounded[:])

        def store_codes(codes, first, count):
            nc.sync.dma_start(out=out_words[:, first : first + count], in_=codes[:].bitcast(I32))

        src01 = placed([P, SLOTS, 2 * BLOCK], F32, "src01", AT_SRC01)
        gather_sources(src01, range(SLOTS), 0, 2 * BLOCK)
        sum01 = sbuf([P, SLOTS, 2 * BLOCK], F32, "sum01")
        last = SLOTS - 1
        for t in range(last):
            add_targets(sum01[:, t, :], t, src01[:, t, :], 0, 2 * BLOCK)
        for first in (0, BLOCK):
            cols = slice(first, first + BLOCK)
            add_targets(sum01[:, last, cols], last, src01[:, last, cols], first, BLOCK)
        w3q = quantize("w3", w3_dealt, H)
        relu0 = placed([P, SLOTS * BLOCK], BF16, "relu0", AT_RELU0)
        relu1 = placed([P, SLOTS * BLOCK], BF16, "relu1", AT_RELU1)
        nc.scalar.activation(*interleaving(relu0[:], sum01[:, :, 0:BLOCK]), RELU)
        nc.scalar.activation(*interleaving(relu1[:], sum01[:, :, BLOCK:]), RELU)

        src2_first = placed([P, 1, BLOCK], F32, "src2_first", AT_SRC2_FIRST)
        gather_sources(src2_first, (0,), 2 * BLOCK, BLOCK)
        z0q = quantize("z0", relu0, BLOCK, tag="dealt")
        src2_middle = placed([P, 2, BLOCK], F32, "src2_middle", AT_SRC2_MIDDLE)
        gather_sources(src2_middle, (1, 2), 2 * BLOCK, BLOCK)
        z1q = quantize("z1", relu1, BLOCK)
        src2_last = placed([P, 1, BLOCK], F32, "src2_last", AT_SRC2_LAST)
        gather_sources(src2_last, (3,), 2 * BLOCK, BLOCK)
        rounded01 = sbuf([P, SLOTS * 2 * BLOCK], BF16, "rounded01")
        for block, zq in enumerate((z0q, z1q)):
            result = sbuf([P, SLOTS, BLOCK], F32, "result%d" % block)
            for n in range(2):
                second_layer_part(zq, n, result, rounded01[:, SLOTS * BLOCK * block : SLOTS * BLOCK * (block + 1)])
            store_result(result, BLOCK * block, BLOCK, nc.sync)
        sum2 = placed([P, SLOTS, BLOCK], F32, "sum2", AT_SUM2)
        src2 = (src2_first[:, 0, :], src2_middle[:, 0, :], src2_middle[:, 1, :], src2_last[:, 0, :])
        for t in range(SLOTS):
            add_targets(sum2[:, t, :], t, src2[t], 2 * BLOCK, BLOCK)
        relu2 = placed([P, SLOTS * BLOCK], BF16, "relu2", AT_RELU2)
        nc.scalar.activation(*interleaving(relu2[:], sum2[:]), RELU)

        first_a, first_b = 3 * BLOCK, 3 * BLOCK + PART
        src3_first = placed([P, 3, BLOCK], F32, "src3_first", AT_SRC3_FIRST)
        gather_sources(src3_first, (0, 1, 2), first_a, BLOCK)
        z2q = quantize("z2", relu2, BLOCK)
        src3_last = placed([P, 1, BLOCK], F32, "src3_last", AT_SRC3_LAST)
        gather_sources(src3_last, (3,), first_a, BLOCK)
        src3 = (src3_first[:, 0, :], src3_first[:, 1, :], src3_first[:, 2, :], src3_last[:, 0, :])
        sum3a = placed([P, SLOTS, PART], F32, "sum3a", AT_SUM3A)
        for t in range(SLOTS):
            add_targets(sum3a[:, t, :], t, src3[t][:, 0:PART], first_a, PART)
        sum3b = placed([P, SLOTS * PART], F32, "sum3b", AT_SUM3B)
        relu3a = sum3b[:, 2 * PART :].bitcast(BF16)
        for t in (0, 1):
            add_targets(sum3b[:, PART * t : PART * (t + 1)], t, src3[t][:, PART:], first_b, PART)
        rounded2 = sbuf([P, SLOTS * BLOCK], BF16, "rounded2")
        result2 = sbuf([P, SLOTS, BLOCK], F32, "result2")
        second_layer_part(z2q, 0, result2, rounded2)
        nc.scalar.activation(*interleaving(relu3a, sum3a[:]), RELU)
        second_layer_part(z2q, 1, result2, rounded2)
        store_result(result2, 2 * BLOCK, BLOCK, nc.sync)
        z3aq = quantize("z3a", relu3a, PART)
        for t in (2, 3):
            add_targets(sum3b[:, PART * t : PART * (t + 1)], t, src3[t][:, PART:], first_b, PART)
        relu3b = placed([P, SLOTS * PART], BF16, "relu3b", AT_RELU3B)
        nc.vector.tensor_scalar_max(*interleaving(relu3b[:], sum3b[:].rearrange("p (t n) -> p t n", t=SLOTS)), 0.0)
        z3bq = quantize("z3b", relu3b, PART)

        codes012 = placed([P, 3 * BLOCK], U32, "codes012", AT_CODES012)
        quantize_out(codes012[:, 0 : 2 * BLOCK], rounded01, 0, 2 * BLOCK)
        quantize_out(codes012[:, 2 * BLOCK :], rounded2, 2 * BLOCK, BLOCK)
        store_codes(codes012, 0, 3 * BLOCK)
        rounded3 = sbuf([P, SLOTS * BLOCK], BF16, "rounded3")
        for n, (zq, first, queue) in enumerate(((z3aq, first_a, nc.sync), (z3bq, first_b, nc.scalar))):
            result = sbuf([P, SLOTS, PART], F32, "result3_%d" % n)
            second_layer(zq, 0, result[:], rounded3[:, SLOTS * PART * n : SLOTS * PART * (n + 1)])
            store_result(result, first, PART, queue)
        codes3 = sbuf([P, BLOCK], U32, "codes3")
        quantize_out(codes3[:], rounded3, first_a, BLOCK)
        store_codes(codes3, first_a, BLOCK)
        for q, queue in enumerate((nc.sync, nc.sync, nc.scalar, nc.scalar)):
            queue.dma_start(out=out_scale_rows[4 * q : 4 * q + 4, :], in_=out_scales[32 * q : 32 * q + 4, :].bitcast(I32))
